import numpy as np
import ml_dtypes


def mxq(x, axis, fmt="e4m3"):
    dtype, down = {"e4m3": (ml_dtypes.float8_e4m3fn, 7), "e5m2": (ml_dtypes.float8_e5m2, 14)}[fmt]
    v = np.moveaxis(np.asarray(x, np.float32).astype(ml_dtypes.bfloat16).astype(np.float64), axis, -1)
    blocks = v.reshape(v.shape[:-1] + (-1, 32))
    amax = np.abs(blocks).max(-1, keepdims=True)
    byte = np.maximum(np.where(amax > 0, np.frexp(amax)[1] - 1 + 127, 0) - down, 1)
    scale = np.exp2(byte - 127.0)
    codes = (blocks / scale).astype(np.float32).astype(dtype).astype(np.float64)
    return np.moveaxis((codes * scale).reshape(v.shape), -1, axis)


WIDE = False


def mx_kscale(k):
    if not WIDE:
        return np.ones(k)
    levels = np.array([10, -10, 5, -5, 0])
    if k % 512:
        return np.exp2(np.random.permutation(np.resize(levels, k // 32))).repeat(32)
    a = np.empty((k // 512, 16))
    for p in range(k // 512):
        a[p, :8] = np.random.permutation(np.resize(levels, 8))
        for g in range(8):
            far = levels[np.abs(levels - a[p, g]) >= 10]
            a[p, g + 8] = far[np.random.randint(len(far))]
    return np.exp2(a.ravel()).repeat(32)


def f64(x):
    return np.asarray(x).astype(np.float64)


def striped(idx):
    return np.tile(idx.reshape(-1, 16).T, (8, 1)).astype(np.uint16)


def unstriped(offs):
    return offs[:16].T.reshape(-1).astype(np.int64)


E2M1 = np.array([0.0, 0.5, 1.0, 1.5, 2.0, 3.0, 4.0, 6.0, -0.0, -0.5, -1.0, -1.5, -2.0, -3.0, -4.0, -6.0])


def pack_weight(w, fmt):
    k, n = w.shape
    w = f64(np.asarray(w, np.float32).astype(ml_dtypes.bfloat16)).reshape(k // 32, 32, n)
    amax = np.abs(w).max(1)
    if fmt == "e4m3":
        byte = np.frexp(amax)[1] - 1 + 127 - 7
    else:
        mant, ex = np.frexp(amax / 6.0)
        byte = np.where(mant > 0.5, ex, ex - 1) + 127
    byte = np.clip(np.where(amax > 0, byte, 1), 1, 254)
    scaled = (w * np.exp2(127.0 - byte)[:, None, :]).reshape(k, n).astype(np.float32)
    by_word = np.ascontiguousarray(scaled.reshape(k // 512, 128, 4, n).transpose(0, 1, 3, 2))
    if fmt == "e4m3":
        words = by_word.astype(ml_dtypes.float8_e4m3fn).view(np.uint8)
    else:
        c = by_word.astype(ml_dtypes.float4_e2m1fn).view(np.uint8) & 0xF
        words = (c[..., 0::2] | (c[..., 1::2] << 4)).reshape(k // 512, 128, 2 * n)
    return np.ascontiguousarray(words), np.ascontiguousarray(byte.astype(np.uint8).reshape(k // 512, 16, n))


def unpack_weight(words, scales, fmt):
    g, _, n = scales.shape
    words = np.ascontiguousarray(words).reshape(g, 128, n, -1)
    if fmt == "e4m3":
        vals = words.view(ml_dtypes.float8_e4m3fn).astype(np.float64)
    else:
        nib = np.empty((g, 128, n, 4), np.uint8)
        nib[..., 0::2] = words & 0xF
        nib[..., 1::2] = words >> 4
        vals = E2M1[nib]
    vals = vals * np.repeat(np.exp2(scales.astype(np.float64) - 127.0), 8, axis=1)[..., None]
    return vals.transpose(0, 1, 3, 2).reshape(g * 512, n)


def gelu(v):
    return 0.5 * v * (1.0 + np.tanh(np.sqrt(2.0 / np.pi) * (v + 0.044715 * v**3)))


K, H, T, S, T2, P = 1536, 1024, 4096, 1024, 2048, 1024

def setup_inputs():
    n = np.random.standard_normal
    s = mx_kscale(K)[:, None]
    u = mx_kscale(H)[:, None]
    d = {}
    d["tab_words"], d["tab_scales"] = pack_weight(n((K, T)) * s, "e4m3")
    d["offs"] = striped(np.random.permutation(T)[:S])
    d["offs2"] = striped(np.random.permutation(T2)[:S])
    d["offs3"] = striped(np.random.permutation(T2)[:P])
    d["offs4"] = striped(np.random.permutation(T2)[:P])
    d["w1"] = (1.5 * n((K, H)) / s / K ** 0.5).astype(np.float32)
    d["gain"] = (2.0 * n(H) * u[:, 0]).astype(np.float32)
    d["wgs"] = np.exp(0.3 * n((128, S))).astype(np.float32)
    d["page0"] = (n((H, T2)) * u).astype(np.float32)
    d["usual"] = (0.8 * n((H, P)) * u).astype(np.float32)
    d["w4_words"], d["w4_scales"] = pack_weight(n((H, H)) / u / H ** 0.5, "e2m1")
    d["moon"] = (0.8 * np.exp(0.3 * n(H)) / u[:, 0]).astype(np.float32)
    return d

def reference(tab_words, tab_scales, offs, offs2, offs3, offs4, w1, gain, wgs, page0, usual, w4_words, w4_scales, moon):
    v = unpack_weight(tab_words, tab_scales, "e4m3")[:, unstriped(offs)]
    w4 = unpack_weight(w4_words, w4_scales, "e2m1")
    f = mxq(f64(w1), 0, "e4m3").T @ v
    h = f64(gain)[:, None] / (1.0 + np.abs(f))
    page = f64(page0).copy()
    page[:, unstriped(offs2)] = np.tile(f64(wgs), (H // 128, 1)) * h
    x = page[:, unstriped(offs3)] - f64(usual)
    y = w4.T @ mxq(x, 0, "e4m3")
    dark = page[:, unstriped(offs4)] * f64(moon)[:, None]
    return (y - dark) * dark

@@ -1,0 +1,241 @@
+from contextlib import ExitStack
+
+import concourse.mybir as mybir
+
+K, H, T, S, T2, NP = 1536, 1024, 4096, 1024, 2048, 1024
+FLOPS = 2 * K * H * S + 2 * H * H * NP
+
+F32 = mybir.dt.float32
+BF16 = mybir.dt.bfloat16
+I32 = mybir.dt.int32
+U32 = mybir.dt.uint32
+U16 = mybir.dt.uint16
+U8 = mybir.dt.uint8
+FP8X4 = mybir.dt.float8_e4m3fn_x4
+FP4X4 = mybir.dt.float4_e2m1fn_x4
+ALU = mybir.AluOpType
+ACT = mybir.ActivationFunctionType
+
+P = 128
+PACK = 4
+BANK = 512
+K_PASSES = K // (P * PACK)
+R_PASSES = H // (P * PACK)
+SLICES = H // P
+W1_GROUPS = (128, 128, 128, 128, 256, 256)
+EARLY = 2
+
+
+def tile_list_eel_passage_ledger_kernel(
+    tc, tab_words, tab_scales, offs, offs2, offs3, offs4, w1, gain, wgs, page0, usual, w4_words, w4_scales, moon, out
+):
+    nc = tc.nc
+    with ExitStack() as ctx:
+        keep = ctx.enter_context(tc.tile_pool(name="keep", bufs=1))
+        work = ctx.enter_context(tc.tile_pool(name="work", bufs=2))
+        psum = ctx.enter_context(tc.psum_pool(name="psum", bufs=4))
+
+        def entries(lst, first, count):
+            if count == 16 * lst.shape[1]:
+                return lst[:]
+            return lst[:, first // 16 : (first + count) // 16]
+
+        idx1 = keep.tile([P, S // 16], U16, name="idx1")
+        idx2 = keep.tile([P, S // 16], U16, name="idx2")
+        idx3 = keep.tile([P, NP // 16], U16, name="idx3")
+        idx4 = keep.tile([P, NP // 16], U16, name="idx4")
+        nc.sync.dma_start(idx1[:], offs)
+
+        warm = keep.tile([P, 8], F32, name="warm")
+        warm2 = keep.tile([P, 8], F32, name="warm2")
+        nc.vector.memset(warm[:], 1.0)
+        nc.scalar.activation(warm2[:], warm[:], ACT.Abs_reciprocal_sqrt)
+
+        tab_planes = work.tile([P, T], U8, name="tab_planes", tag="x")
+        nc.vector.memset(tab_planes[:].bitcast(I32), 0)
+
+        w1_codes = {}
+        w1_planes = {}
+
+        w1_raw = {}
+
+        def load_w1(group, passes=range(K_PASSES)):
+            first = sum(W1_GROUPS[:group])
+            width = W1_GROUPS[group]
+            if group not in w1_raw:
+                shape = [P, K_PASSES, PACK, width]
+                if width == P:
+                    w1_raw[group] = work.tile(shape, F32, name="w1_narrow", bufs=4)
+                elif group == len(W1_GROUPS) - 1:
+                    w1_raw[group] = work.tile(shape, F32, name="w1_last", tag="big", bufs=3, align_bytes=64)
+                else:
+                    w1_raw[group] = work.tile(shape, F32, name="w1_wide", tag="wide", bufs=1)
+            for a in passes:
+                rows = w1[a * P * PACK : (a + 1) * P * PACK, first : first + width]
+                nc.sync.dma_start(w1_raw[group][:, a], rows.rearrange("(p j) c -> p j c", j=PACK))
+
+        def quantize_w1(group):
+            first = sum(W1_GROUPS[:group])
+            width = W1_GROUPS[group]
+            woven = work.tile([P, K_PASSES, width, PACK], BF16, name="w1_woven", tag="woven", align_bytes=64)
+            for a in range(K_PASSES):
+                nc.scalar.copy(woven[:, a], w1_raw[group][:, a].rearrange("p j c -> p c j"))
+                codes = keep.tile([P, width], U32, name="w1_codes_%d_%d" % (group, a), align_bytes=64)
+                plane = keep.tile([P, width], U8, name="w1_plane_%d_%d" % (group, a), align_bytes=64)
+                nc.vector.quantize_mx(codes[:].bitcast(FP8X4), plane[:], woven[:, a].rearrange("p c j -> p (c j)"))
+                for c in range(0, width, P):
+                    w1_codes[(first + c) // P, a] = codes[:, c : c + P]
+                    w1_planes[(first + c) // P, a] = plane[:, c : c + P]
+
+        windows = []
+        for a in range(K_PASSES):
+            window = work.tile([P, T], I32, name="window", tag="big", bufs=3, align_bytes=64)
+            nc.sync.dma_start(window[:], tab_words[a].rearrange("p t i -> p (t i)").bitcast(I32))
+            if a == 0:
+                for quad in range(4):
+                    nc.sync.dma_start(
+                        tab_planes[32 * quad : 32 * quad + 4 * K_PASSES, :].bitcast(I32),
+                        tab_scales[:, 4 * quad : 4 * quad + 4, :].bitcast(I32),
+                    )
+            load_w1(0, (a,))
+            windows.append(window)
+        quantize_w1(0)
+        v_codes = {}
+        v_planes = keep.tile([P, S], U8, name="v_planes", align_bytes=64)
+        for a in range(K_PASSES):
+            if a == 1:
+                nc.vector.tensor_copy(v_planes[:], tab_planes[:].indirect(idx1[:]))
+            for c in range(0, S, BANK):
+                picked = keep.tile([P, BANK], U32, name="v_codes_%d_%d" % (a, c), align_bytes=64)
+                nc.vector.tensor_copy(picked[:], windows[a][:].bitcast(U32).indirect(entries(idx1, c, BANK)))
+                v_codes[a, c] = picked
+
+        nc.sync.dma_start(idx2[:], offs2)
+        wgs_sb = keep.tile([P, S], F32, name="wgs_sb")
+        gain_sb = keep.tile([P, SLICES], F32, name="gain_sb")
+        moon_sb = keep.tile([P, SLICES], F32, name="moon_sb")
+        neg_moon = keep.tile([P, SLICES], F32, name="neg_moon")
+        with nc.allow_non_contiguous_dma(reason="one value for each row of a slice"):
+            nc.scalar.dma_start(gain_sb[:], gain.rearrange("(i p) -> p i", p=P))
+        pages = []
+        early = []
+        x_codes = keep.tile([P, R_PASSES, NP], U32, name="x_codes", align_bytes=64)
+        x_planes = keep.tile([P, R_PASSES, NP], U8, name="x_planes", align_bytes=64)
+        w4_sb = keep.tile([P, R_PASSES, 2 * H], U8, name="w4_sb", align_bytes=64)
+        w4_planes = keep.tile([P, R_PASSES, H], U8, name="w4_planes", align_bytes=64)
+
+        def put(i, first, count):
+            h = work.tile([P, count], F32, name="h", bufs=3)
+            for c in range(first, first + count, BANK):
+                n = min(count, BANK)
+                half, start = divmod(c, BANK)
+                f = psum.tile([P, n], F32, name="f")
+                for a in range(K_PASSES):
+                    nc.tensor.matmul_mx(
+                        out=f[:],
+                        lhsT=w1_codes[i, a].bitcast(FP8X4),
+                        lhsT_scale=w1_planes[i, a],
+                        rhs=v_codes[a, half * BANK][:, start : start + n].bitcast(FP8X4),
+                        rhs_scale=v_planes[4 * a :, c : c + n],
+                        start=(a == 0),
+                        stop=(a == K_PASSES - 1),
+                    )
+                nc.scalar.activation(h[:, c - first : c - first + n], f[:], ACT.Abs)
+            nc.scalar.activation(h[:], h[:], ACT.Abs_reciprocal_sqrt, bias=1.0)
+            nc.scalar.activation(h[:], h[:], ACT.Square)
+            nc.scalar.activation(h[:], h[:], ACT.Copy, scale=gain_sb[:, i : i + 1])
+            nc.vector.tensor_tensor(
+                pages[i][:].indirect(entries(idx2, first, count)), h[:], wgs_sb[:, first : first + count], ALU.mult
+            )
+
+        def quantize_x(b, dealt, first, count):
+            woven = work.tile([P, count, PACK], BF16, name="x_woven", tag="woven", align_bytes=64)
+            nc.scalar.copy(woven[:], dealt[:, :, first : first + count].rearrange("p j c -> p c j"))
+            nc.vector.quantize_mx(
+                x_codes[:, b, first : first + count].bitcast(FP8X4),
+                x_planes[:, b, first : first + count],
+                woven[:].rearrange("p c j -> p (c j)"),
+            )
+
+        with tc.tile_pool(name="usual_pool", bufs=3) as usual_pool:
+            for i in range(SLICES):
+                b, quad = divmod(i, PACK)
+                if i < 4:
+                    page = keep.tile([P, T2], F32, name="page_%d" % i)
+                elif i == 6:
+                    page = work.tile([P, T2], F32, name="page_%d" % i, tag="wide", bufs=1)
+                else:
+                    page = work.tile([P, T2], F32, name="page_%d" % i, tag="big", bufs=3, align_bytes=64)
+                pages.append(page)
+                if i in (1, 2):
+                    load_w1(2 * i)
+                nc.sync.dma_start(pages[i][:], page0[i * P : (i + 1) * P, :])
+                if i == 0:
+                    for half in range(2):
+                        nc.sync.dma_start(wgs_sb[:, half * BANK : (half + 1) * BANK], wgs[:, half * BANK : (half + 1) * BANK])
+                    nc.sync.dma_start(idx3[:], offs3)
+                    nc.sync.dma_start(idx4[:], offs4)
+                if i in (0, 1, 3):
+                    load_w1({0: 1, 1: 3, 3: 5}[i])
+                usual_sb = usual_pool.tile([P, NP], F32, name="usual_sb")
+                nc.sync.dma_start(usual_sb[:], usual[i * P : (i + 1) * P, :])
+                if i == SLICES - 2:
+                    nc.sync.dma_start(w4_sb[:].bitcast(I32), w4_words.rearrange("a p c -> p a c").bitcast(I32))
+                    nc.vector.memset(w4_planes[:].bitcast(I32), 0)
+                    for q in range(4):
+                        nc.sync.dma_start(
+                            w4_planes[32 * q : 32 * q + 4, :, :].bitcast(I32),
+                            w4_scales[:, 4 * q : 4 * q + 4, :].rearrange("a r c -> r a c").bitcast(I32),
+                        )
+                    with nc.allow_non_contiguous_dma(reason="one value for each row of a slice"):
+                        nc.sync.dma_start(moon_sb[:], moon.rearrange("(i p) -> p i", p=P))
+                    nc.scalar.mul(neg_moon[:], moon_sb[:], -1.0)
+                pieces = {0: ((0, 256), (256, 256), (512, 512)), 1: ((0, BANK), (BANK, BANK))}.get(i, ((0, S),))
+                for first, count in pieces:
+                    put(i, first, count)
+                for group in {0: (1,), 1: (2, 3), 2: (4,), 3: (5,)}.get(i, ()):
+                    quantize_w1(group)
+                if quad == 0:
+                    dealt = work.tile([P, PACK, NP], F32, name="dealt", bufs=1)
+                pieces = ((0, BANK), (BANK, BANK)) if i == SLICES - 1 else ((0, NP),)
+                queue = nc.sync if i == SLICES - 1 else nc.gpsimd
+                for first, count in pieces:
+                    x = work.tile([P, count], F32, name="x")
+                    nc.vector.tensor_tensor(
+                        x[:], pages[i][:].indirect(entries(idx3, first, count)), usual_sb[:, first : first + count], ALU.subtract
+                    )
+                    queue.dma_start(dealt[32 * quad : 32 * quad + 32, :, first : first + count], x[:])
+                if i < EARLY:
+                    g = keep.tile([P, NP], F32, name="g_%d" % i)
+                    nc.vector.tensor_copy(g[:], pages[i][:].indirect(idx4[:]))
+                    early.append(g)
+                if quad == PACK - 1:
+                    for first in range(0, NP, BANK):
+                        quantize_x(b, dealt, first, BANK)
+
+        with tc.tile_pool(name="tail_pool", bufs=3) as tail_pool:
+            for i in range(SLICES):
+                if i < EARLY:
+                    g = early[i]
+                else:
+                    g = tail_pool.tile([P, NP], F32, name="g")
+                    nc.vector.tensor_copy(g[:], pages[i][:].indirect(idx4[:]))
+                res = work.tile([P, NP], F32, name="res", tag="x")
+                diff = work.tile([P, NP], F32, name="diff", tag="h", bufs=3)
+                for c in range(0, NP, BANK):
+                    y = psum.tile([P, BANK], F32, name="y")
+                    for b in range(R_PASSES):
+                        nc.tensor.matmul_mx(
+                            out=y[:],
+                            lhsT=w4_sb[:, b, 2 * i * P : 2 * (i + 1) * P].bitcast(FP4X4),
+                            lhsT_scale=w4_planes[:, b, i * P : (i + 1) * P],
+                            rhs=x_codes[:, b, c : c + BANK].bitcast(FP8X4),
+                            rhs_scale=x_planes[:, b, c : c + BANK],
+                            start=(b == 0),
+                            stop=(b == R_PASSES - 1),
+                        )
+                    nc.vector.scalar_tensor_tensor(
+                        diff[:, c : c + BANK], g[:, c : c + BANK], neg_moon[:, i : i + 1], y[:], ALU.mult, ALU.add
+                    )
+                nc.vector.scalar_tensor_tensor(res[:], g[:], moon_sb[:, i : i + 1], diff[:], ALU.mult, ALU.mult)
+                nc.sync.dma_start(out[i * P : (i + 1) * P, :], res[:])

@@ -23,7 +23,11 @@ K_PASSES = K // (P * PACK)
 R_PASSES = H // (P * PACK)
 SLICES = H // P
 W1_GROUPS = (128, 128, 128, 128, 256, 256)
-EARLY = 2
+LOADS = {0: (1, 2), 1: (3,), 2: (4,), 3: (5,)}
+QUANTS = {0: (1, 2), 1: (3,), 2: (4,), 3: (5,)}
+EARLY = 1
+TAIL_PICKS = 6
+LAST_ON_VECTOR = 2
 
 
 def tile_list_eel_passage_ledger_kernel(
@@ -36,9 +40,18 @@ def tile_list_eel_passage_ledger_kernel(
         psum = ctx.enter_context(tc.psum_pool(name="psum", bufs=4))
 
         def entries(lst, first, count):
-            if count == 16 * lst.shape[1]:
-                return lst[:]
             return lst[:, first // 16 : (first + count) // 16]
+
+        def big(shape, dtype, name):
+            return work.tile(shape, dtype, name=name, tag="big", bufs=3)
+
+        def mid(shape, dtype, name):
+            return work.tile(shape, dtype, name=name, tag="mid", bufs=4)
+
+        def weave(woven, rows):
+            nc.scalar.copy(
+                woven.rearrange("p (c i) j -> p c j i", i=PACK), rows.rearrange("p j (c i) -> p c j i", i=PACK)
+            )
 
         idx1 = keep.tile([P, S // 16], U16, name="idx1")
         idx2 = keep.tile([P, S // 16], U16, name="idx2")
@@ -54,131 +67,126 @@ def tile_list_eel_passage_ledger_kernel(
         tab_planes = work.tile([P, T], U8, name="tab_planes", tag="x")
         nc.vector.memset(tab_planes[:].bitcast(I32), 0)
 
-        w1_codes = {}
-        w1_planes = {}
-
-        w1_raw = {}
-
-        def load_w1(group, passes=range(K_PASSES)):
-            first = sum(W1_GROUPS[:group])
-            width = W1_GROUPS[group]
-            if group not in w1_raw:
-                shape = [P, K_PASSES, PACK, width]
-                if width == P:
-                    w1_raw[group] = work.tile(shape, F32, name="w1_narrow", bufs=4)
-                elif group == len(W1_GROUPS) - 1:
-                    w1_raw[group] = work.tile(shape, F32, name="w1_last", tag="big", bufs=3, align_bytes=64)
-                else:
-                    w1_raw[group] = work.tile(shape, F32, name="w1_wide", tag="wide", bufs=1)
-            for a in passes:
-                rows = w1[a * P * PACK : (a + 1) * P * PACK, first : first + width]
-                nc.sync.dma_start(w1_raw[group][:, a], rows.rearrange("(p j) c -> p j c", j=PACK))
-
-        def quantize_w1(group):
-            first = sum(W1_GROUPS[:group])
-            width = W1_GROUPS[group]
-            woven = work.tile([P, K_PASSES, width, PACK], BF16, name="w1_woven", tag="woven", align_bytes=64)
-            for a in range(K_PASSES):
-                nc.scalar.copy(woven[:, a], w1_raw[group][:, a].rearrange("p j c -> p c j"))
-                codes = keep.tile([P, width], U32, name="w1_codes_%d_%d" % (group, a), align_bytes=64)
-                plane = keep.tile([P, width], U8, name="w1_plane_%d_%d" % (group, a), align_bytes=64)
-                nc.vector.quantize_mx(codes[:].bitcast(FP8X4), plane[:], woven[:, a].rearrange("p c j -> p (c j)"))
-                for c in range(0, width, P):
-                    w1_codes[(first + c) // P, a] = codes[:, c : c + P]
-                    w1_planes[(first + c) // P, a] = plane[:, c : c + P]
-
-        windows = []
-        for a in range(K_PASSES):
-            window = work.tile([P, T], I32, name="window", tag="big", bufs=3, align_bytes=64)
-            nc.sync.dma_start(window[:], tab_words[a].rearrange("p t i -> p (t i)").bitcast(I32))
-            if a == 0:
-                for quad in range(4):
-                    nc.sync.dma_start(
-                        tab_planes[32 * quad : 32 * quad + 4 * K_PASSES, :].bitcast(I32),
-                        tab_scales[:, 4 * quad : 4 * quad + 4, :].bitcast(I32),
-                    )
-            load_w1(0, (a,))
-            windows.append(window)
-        quantize_w1(0)
-        v_codes = {}
-        v_planes = keep.tile([P, S], U8, name="v_planes", align_bytes=64)
-        for a in range(K_PASSES):
-            if a == 1:
-                nc.vector.tensor_copy(v_planes[:], tab_planes[:].indirect(idx1[:]))
-            for c in range(0, S, BANK):
-                picked = keep.tile([P, BANK], U32, name="v_codes_%d_%d" % (a, c), align_bytes=64)
-                nc.vector.tensor_copy(picked[:], windows[a][:].bitcast(U32).indirect(entries(idx1, c, BANK)))
-                v_codes[a, c] = picked
-
-        nc.sync.dma_start(idx2[:], offs2)
-        wgs_sb = keep.tile([P, S], F32, name="wgs_sb")
         gain_sb = keep.tile([P, SLICES], F32, name="gain_sb")
         moon_sb = keep.tile([P, SLICES], F32, name="moon_sb")
         neg_moon = keep.tile([P, SLICES], F32, name="neg_moon")
         with nc.allow_non_contiguous_dma(reason="one value for each row of a slice"):
             nc.scalar.dma_start(gain_sb[:], gain.rearrange("(i p) -> p i", p=P))
-        pages = []
-        early = []
+        wgs_sb = keep.tile([P, S], F32, name="wgs_sb")
+        v_planes = keep.tile([P, S], U8, name="v_planes", align_bytes=64)
         x_codes = keep.tile([P, R_PASSES, NP], U32, name="x_codes", align_bytes=64)
         x_planes = keep.tile([P, R_PASSES, NP], U8, name="x_planes", align_bytes=64)
         w4_sb = keep.tile([P, R_PASSES, 2 * H], U8, name="w4_sb", align_bytes=64)
         w4_planes = keep.tile([P, R_PASSES, H], U8, name="w4_planes", align_bytes=64)
+        w1_raw = {}
+        w1_codes = {}
+        w1_planes = {}
+        v_codes = {}
+        pages = []
+        dealt = []
+        picks = {}
 
-        def put(i, first, count):
-            h = work.tile([P, count], F32, name="h", bufs=3)
-            for c in range(first, first + count, BANK):
-                n = min(count, BANK)
-                half, start = divmod(c, BANK)
-                f = psum.tile([P, n], F32, name="f")
+        with tc.tile_pool(name="main_pool", bufs=2) as main_pool:
+
+            def load_w1(group, passes=range(K_PASSES)):
+                first, width = sum(W1_GROUPS[:group]), W1_GROUPS[group]
+                if group not in w1_raw:
+                    shape = [P, K_PASSES, PACK, width]
+                    if width == P:
+                        w1_raw[group] = mid(shape, F32, "w1_narrow")
+                    else:
+                        w1_raw[group] = big(shape, F32, "w1_raw_%d" % group)
+                for a in passes:
+                    rows = w1[a * P * PACK : (a + 1) * P * PACK, first : first + width]
+                    nc.sync.dma_start(w1_raw[group][:, a], rows.rearrange("(p j) c -> p j c", j=PACK))
+
+            def quantize_w1(group):
+                first, width = sum(W1_GROUPS[:group]), W1_GROUPS[group]
+                woven = main_pool.tile([P, K_PASSES, width, PACK], BF16, name="w1_woven", align_bytes=64)
                 for a in range(K_PASSES):
-                    nc.tensor.matmul_mx(
-                        out=f[:],
-                        lhsT=w1_codes[i, a].bitcast(FP8X4),
-                        lhsT_scale=w1_planes[i, a],
-                        rhs=v_codes[a, half * BANK][:, start : start + n].bitcast(FP8X4),
-                        rhs_scale=v_planes[4 * a :, c : c + n],
-                        start=(a == 0),
-                        stop=(a == K_PASSES - 1),
+                    weave(woven[:, a], w1_raw[group][:, a])
+                    codes = keep.tile([P, width], U32, name="w1_codes_%d_%d" % (group, a), align_bytes=64)
+                    plane = keep.tile([P, width], U8, name="w1_plane_%d_%d" % (group, a), align_bytes=64)
+                    nc.vector.quantize_mx(codes[:].bitcast(FP8X4), plane[:], woven[:, a].rearrange("p c j -> p (c j)"))
+                    for c in range(0, width, P):
+                        w1_codes[(first + c) // P, a] = codes[:, c : c + P]
+                        w1_planes[(first + c) // P, a] = plane[:, c : c + P]
+
+            def put(i, first, count):
+                h = work.tile([P, count], F32, name="h", bufs=3)
+                for c in range(first, first + count, BANK):
+                    n = min(count, BANK)
+                    half, start = divmod(c, BANK)
+                    f = psum.tile([P, n], F32, name="f")
+                    for a in range(K_PASSES):
+                        nc.tensor.matmul_mx(
+                            out=f[:],
+                            lhsT=w1_codes[i, a].bitcast(FP8X4),
+                            lhsT_scale=w1_planes[i, a],
+                            rhs=v_codes[a, half][:, start : start + n].bitcast(FP8X4),
+                            rhs_scale=v_planes[4 * a :, c : c + n],
+                            start=(a == 0),
+                            stop=(a == K_PASSES - 1),
+                        )
+                    nc.scalar.activation(h[:, c - first : c - first + n], f[:], ACT.Abs)
+                parts = [h[:, c : c + BANK] for c in range(0, count, BANK)] if count > BANK else [h[:]]
+                for part in parts:
+                    nc.scalar.activation(part, part, ACT.Abs_reciprocal_sqrt, bias=1.0)
+                for part in parts:
+                    nc.scalar.activation(part, part, ACT.Square)
+                for part in parts:
+                    nc.scalar.activation(part, part, ACT.Copy, scale=gain_sb[:, i : i + 1])
+                nc.vector.tensor_tensor(
+                    pages[i][:].indirect(entries(idx2, first, count)), h[:], wgs_sb[:, first : first + count], ALU.mult
+                )
+
+            windows = []
+            for a in range(K_PASSES):
+                if a == K_PASSES - 1:
+                    load_w1(0, (1, 2))
+                window = big([P, T], I32, "window")
+                nc.sync.dma_start(window[:], tab_words[a].rearrange("p t i -> p (t i)").bitcast(I32))
+                windows.append(window)
+                if a == 0:
+                    for quad in range(4):
+                        nc.sync.dma_start(
+                            tab_planes[32 * quad : 32 * quad + 4 * K_PASSES, :].bitcast(I32),
+                            tab_scales[:, 4 * quad : 4 * quad + 4, :].bitcast(I32),
+                        )
+                    load_w1(0, (0,))
+            quantize_w1(0)
+            for a in range(K_PASSES):
+                if a == 1:
+                    nc.vector.tensor_copy(v_planes[:], tab_planes[:].indirect(idx1[:]))
+                for half in range(S // BANK):
+                    picked = keep.tile([P, BANK], U32, name="v_codes_%d_%d" % (a, half), align_bytes=64)
+                    nc.vector.tensor_copy(
+                        picked[:], windows[a][:].bitcast(U32).indirect(entries(idx1, half * BANK, BANK))
                     )
-                nc.scalar.activation(h[:, c - first : c - first + n], f[:], ACT.Abs)
-            nc.scalar.activation(h[:], h[:], ACT.Abs_reciprocal_sqrt, bias=1.0)
-            nc.scalar.activation(h[:], h[:], ACT.Square)
-            nc.scalar.activation(h[:], h[:], ACT.Copy, scale=gain_sb[:, i : i + 1])
-            nc.vector.tensor_tensor(
-                pages[i][:].indirect(entries(idx2, first, count)), h[:], wgs_sb[:, first : first + count], ALU.mult
-            )
+                    v_codes[a, half] = picked
+            nc.sync.dma_start(idx2[:], offs2)
 
-        def quantize_x(b, dealt, first, count):
-            woven = work.tile([P, count, PACK], BF16, name="x_woven", tag="woven", align_bytes=64)
-            nc.scalar.copy(woven[:], dealt[:, :, first : first + count].rearrange("p j c -> p c j"))
-            nc.vector.quantize_mx(
-                x_codes[:, b, first : first + count].bitcast(FP8X4),
-                x_planes[:, b, first : first + count],
-                woven[:].rearrange("p c j -> p (c j)"),
-            )
-
-        with tc.tile_pool(name="usual_pool", bufs=3) as usual_pool:
             for i in range(SLICES):
                 b, quad = divmod(i, PACK)
                 if i < 4:
                     page = keep.tile([P, T2], F32, name="page_%d" % i)
-                elif i == 6:
-                    page = work.tile([P, T2], F32, name="page_%d" % i, tag="wide", bufs=1)
+                elif i < 6:
+                    page = mid([P, T2], F32, "page_%d" % i)
                 else:
-                    page = work.tile([P, T2], F32, name="page_%d" % i, tag="big", bufs=3, align_bytes=64)
+                    page = big([P, T2], F32, "page_%d" % i)
                 pages.append(page)
-                if i in (1, 2):
-                    load_w1(2 * i)
                 nc.sync.dma_start(pages[i][:], page0[i * P : (i + 1) * P, :])
                 if i == 0:
-                    for half in range(2):
-                        nc.sync.dma_start(wgs_sb[:, half * BANK : (half + 1) * BANK], wgs[:, half * BANK : (half + 1) * BANK])
+                    for c in range(0, S, BANK):
+                        nc.sync.dma_start(wgs_sb[:, c : c + BANK], wgs[:, c : c + BANK])
+                for group in LOADS.get(i, ()):
+                    load_w1(group)
+                usual_sb = main_pool.tile([P, NP], F32, name="usual_sb", bufs=3)
+                if i == 0:
                     nc.sync.dma_start(idx3[:], offs3)
-                    nc.sync.dma_start(idx4[:], offs4)
-                if i in (0, 1, 3):
-                    load_w1({0: 1, 1: 3, 3: 5}[i])
-                usual_sb = usual_pool.tile([P, NP], F32, name="usual_sb")
                 nc.sync.dma_start(usual_sb[:], usual[i * P : (i + 1) * P, :])
+                if i == 0:
+                    nc.sync.dma_start(idx4[:], offs4)
                 if i == SLICES - 2:
                     nc.sync.dma_start(w4_sb[:].bitcast(I32), w4_words.rearrange("a p c -> p a c").bitcast(I32))
                     nc.vector.memset(w4_planes[:].bitcast(I32), 0)
@@ -190,39 +198,48 @@ def tile_list_eel_passage_ledger_kernel(
                     with nc.allow_non_contiguous_dma(reason="one value for each row of a slice"):
                         nc.sync.dma_start(moon_sb[:], moon.rearrange("(i p) -> p i", p=P))
                     nc.scalar.mul(neg_moon[:], moon_sb[:], -1.0)
-                pieces = {0: ((0, 256), (256, 256), (512, 512)), 1: ((0, BANK), (BANK, BANK))}.get(i, ((0, S),))
+                pieces = ((0, 256), (256, 256), (512, 512)) if i == 0 else ((0, S),)
                 for first, count in pieces:
                     put(i, first, count)
-                for group in {0: (1,), 1: (2, 3), 2: (4,), 3: (5,)}.get(i, ()):
+                for group in QUANTS.get(i, ()):
                     quantize_w1(group)
-                if quad == 0:
-                    dealt = work.tile([P, PACK, NP], F32, name="dealt", bufs=1)
+                if i == 0:
+                    dealt.append(keep.tile([P, PACK, NP], F32, name="dealt_0"))
+                if i == PACK:
+                    dealt.append(big([P, PACK, NP], F32, "dealt_1"))
                 pieces = ((0, BANK), (BANK, BANK)) if i == SLICES - 1 else ((0, NP),)
                 queue = nc.sync if i == SLICES - 1 else nc.gpsimd
                 for first, count in pieces:
                     x = work.tile([P, count], F32, name="x")
                     nc.vector.tensor_tensor(
-                        x[:], pages[i][:].indirect(entries(idx3, first, count)), usual_sb[:, first : first + count], ALU.subtract
+                        x[:],
+                        pages[i][:].indirect(entries(idx3, first, count)),
+                        usual_sb[:, first : first + count],
+                        ALU.subtract,
                     )
-                    queue.dma_start(dealt[32 * quad : 32 * quad + 32, :, first : first + count], x[:])
+                    queue.dma_start(dealt[b][32 * quad : 32 * quad + 32, :, first : first + count], x[:])
                 if i < EARLY:
                     g = keep.tile([P, NP], F32, name="g_%d" % i)
                     nc.vector.tensor_copy(g[:], pages[i][:].indirect(idx4[:]))
-                    early.append(g)
-                if quad == PACK - 1:
-                    for first in range(0, NP, BANK):
-                        quantize_x(b, dealt, first, BANK)
+                    for c in range(0, NP, BANK):
+                        picks[i, c] = g[:, c : c + BANK]
 
-        with tc.tile_pool(name="tail_pool", bufs=3) as tail_pool:
-            for i in range(SLICES):
-                if i < EARLY:
-                    g = early[i]
-                else:
-                    g = tail_pool.tile([P, NP], F32, name="g")
-                    nc.vector.tensor_copy(g[:], pages[i][:].indirect(idx4[:]))
-                res = work.tile([P, NP], F32, name="res", tag="x")
-                diff = work.tile([P, NP], F32, name="diff", tag="h", bufs=3)
-                for c in range(0, NP, BANK):
+        with tc.tile_pool(name="tail_pool", bufs=2) as tail_pool:
+            for c in range(0, NP, BANK):
+                for b in range(R_PASSES):
+                    woven = tail_pool.tile([P, BANK, PACK], BF16, name="x_woven", bufs=4, align_bytes=64)
+                    weave(woven[:], dealt[b][:, :, c : c + BANK])
+                    nc.vector.quantize_mx(
+                        x_codes[:, b, c : c + BANK].bitcast(FP8X4),
+                        x_planes[:, b, c : c + BANK],
+                        woven[:].rearrange("p c j -> p (c j)"),
+                    )
+            for c in range(0, NP, BANK):
+                for i in range(SLICES):
+                    if (i, c) not in picks:
+                        g = tail_pool.tile([P, BANK], F32, name="g", bufs=TAIL_PICKS)
+                        nc.vector.tensor_copy(g[:], pages[i][:].indirect(entries(idx4, c, BANK)))
+                        picks[i, c] = g[:]
                     y = psum.tile([P, BANK], F32, name="y")
                     for b in range(R_PASSES):
                         nc.tensor.matmul_mx(
@@ -234,8 +251,16 @@ def tile_list_eel_passage_ledger_kernel(
                             start=(b == 0),
                             stop=(b == R_PASSES - 1),
                         )
+                    diff = work.tile([P, BANK], F32, name="diff", tag="h", bufs=3)
                     nc.vector.scalar_tensor_tensor(
-                        diff[:, c : c + BANK], g[:, c : c + BANK], neg_moon[:, i : i + 1], y[:], ALU.mult, ALU.add
+                        diff[:], picks[i, c], neg_moon[:, i : i + 1], y[:], ALU.mult, ALU.add
                     )
-                nc.vector.scalar_tensor_tensor(res[:], g[:], moon_sb[:, i : i + 1], diff[:], ALU.mult, ALU.mult)
-                nc.sync.dma_start(out[i * P : (i + 1) * P, :], res[:])
+                    res = tail_pool.tile([P, BANK], F32, name="res", bufs=4)
+                    if c * SLICES // BANK + i >= 2 * SLICES - LAST_ON_VECTOR:
+                        nc.vector.scalar_tensor_tensor(
+                            res[:], picks[i, c], moon_sb[:, i : i + 1], diff[:], ALU.mult, ALU.mult
+                        )
+                    else:
+                        nc.gpsimd.tensor_tensor(res[:], diff[:], picks[i, c], ALU.mult)
+                        nc.scalar.activation(res[:], res[:], ACT.Copy, scale=moon_sb[:, i : i + 1])
+                    nc.sync.dma_start(out[i * P : (i + 1) * P, c : c + BANK], res[:])

@@ -1,9 +1,10 @@
 from contextlib import ExitStack
 
 import concourse.mybir as mybir
+from concourse.masks import make_identity
 
-K, H, T, S, T2, NP = 1536, 1024, 4096, 1024, 2048, 1024
-FLOPS = 2 * K * H * S + 2 * H * H * NP
+K, H, T, S, T2, M = 1536, 1024, 4096, 1024, 2048, 1024
+FLOPS = 2 * K * H * S + 2 * H * H * M
 
 F32 = mybir.dt.float32
 BF16 = mybir.dt.bfloat16
@@ -18,16 +19,23 @@ ACT = mybir.ActivationFunctionType
 
 P = 128
 PACK = 4
+PASS = P * PACK
 BANK = 512
-K_PASSES = K // (P * PACK)
-R_PASSES = H // (P * PACK)
+QUADRANTS = 4
+LIST_ROWS = 16
+K_PASSES = K // PASS
+R_PASSES = H // PASS
 SLICES = H // P
-W1_GROUPS = (128, 128, 128, 128, 256, 256)
-LOADS = {0: (1, 2), 1: (3,), 2: (4,), 3: (5,)}
-QUANTS = {0: (1, 2), 1: (3,), 2: (4,), 3: (5,)}
-EARLY = 1
-TAIL_PICKS = 6
+
+W1_GROUPS = (P, P, P, P, 2 * P, 2 * P)
+W1_AHEAD = 2
+FIRST_PIECES = ((0, BANK // 2), (BANK // 2, BANK // 2), (BANK, BANK))
+TURN_LAG = 2
+PICK_BUFS = 6
 LAST_ON_VECTOR = 2
+OWN_PAGES = 4
+MID_BUFS = 4
+HELD_SLICES = TURN_LAG + 1
 
 
 def tile_list_eel_passage_ledger_kernel(
@@ -40,32 +48,29 @@ def tile_list_eel_passage_ledger_kernel(
         psum = ctx.enter_context(tc.psum_pool(name="psum", bufs=4))
 
         def entries(lst, first, count):
-            return lst[:, first // 16 : (first + count) // 16]
+            return lst[:, first // LIST_ROWS : (first + count) // LIST_ROWS]
 
         def big(shape, dtype, name):
-            return work.tile(shape, dtype, name=name, tag="big", bufs=3)
+            return work.tile(shape, dtype, name=name, tag="big", bufs=K_PASSES)
 
         def mid(shape, dtype, name):
-            return work.tile(shape, dtype, name=name, tag="mid", bufs=4)
+            return work.tile(shape, dtype, name=name, tag="mid", bufs=MID_BUFS)
 
-        def weave(woven, rows):
-            nc.scalar.copy(
-                woven.rearrange("p (c i) j -> p c j i", i=PACK), rows.rearrange("p j (c i) -> p c j i", i=PACK)
-            )
-
-        idx1 = keep.tile([P, S // 16], U16, name="idx1")
-        idx2 = keep.tile([P, S // 16], U16, name="idx2")
-        idx3 = keep.tile([P, NP // 16], U16, name="idx3")
-        idx4 = keep.tile([P, NP // 16], U16, name="idx4")
+        idx1 = keep.tile([P, S // LIST_ROWS], U16, name="idx1")
+        idx2 = keep.tile([P, S // LIST_ROWS], U16, name="idx2")
+        idx3 = keep.tile([P, M // LIST_ROWS], U16, name="idx3")
+        idx4 = keep.tile([P, M // LIST_ROWS], U16, name="idx4")
         nc.sync.dma_start(idx1[:], offs)
 
-        warm = keep.tile([P, 8], F32, name="warm")
-        warm2 = keep.tile([P, 8], F32, name="warm2")
-        nc.vector.memset(warm[:], 1.0)
-        nc.scalar.activation(warm2[:], warm[:], ACT.Abs_reciprocal_sqrt)
+        ones = keep.tile([P, 8], F32, name="ones")
+        warmed = keep.tile([P, 8], F32, name="warmed")
+        nc.vector.memset(ones[:], 1.0)
+        nc.scalar.activation(warmed[:], ones[:], ACT.Abs_reciprocal_sqrt)
 
-        tab_planes = work.tile([P, T], U8, name="tab_planes", tag="x")
+        tab_planes = work.tile([P, T], U8, name="tab_planes", tag="negated", bufs=HELD_SLICES)
         nc.vector.memset(tab_planes[:].bitcast(I32), 0)
+        identity = keep.tile([P, P], F32, name="identity")
+        make_identity(nc, identity[:])
 
         gain_sb = keep.tile([P, SLICES], F32, name="gain_sb")
         moon_sb = keep.tile([P, SLICES], F32, name="moon_sb")
@@ -74,8 +79,9 @@ def tile_list_eel_passage_ledger_kernel(
             nc.scalar.dma_start(gain_sb[:], gain.rearrange("(i p) -> p i", p=P))
         wgs_sb = keep.tile([P, S], F32, name="wgs_sb")
         v_planes = keep.tile([P, S], U8, name="v_planes", align_bytes=64)
-        x_codes = keep.tile([P, R_PASSES, NP], U32, name="x_codes", align_bytes=64)
-        x_planes = keep.tile([P, R_PASSES, NP], U8, name="x_planes", align_bytes=64)
+        x_turned = [keep.tile([P, M // P, PASS], BF16, name="x_turned_%d" % b) for b in range(R_PASSES)]
+        x_codes = keep.tile([P, R_PASSES, M], U32, name="x_codes", align_bytes=64)
+        x_planes = keep.tile([P, R_PASSES, M], U8, name="x_planes", align_bytes=64)
         w4_sb = keep.tile([P, R_PASSES, 2 * H], U8, name="w4_sb", align_bytes=64)
         w4_planes = keep.tile([P, R_PASSES, H], U8, name="w4_planes", align_bytes=64)
         w1_raw = {}
@@ -83,28 +89,63 @@ def tile_list_eel_passage_ledger_kernel(
         w1_planes = {}
         v_codes = {}
         pages = []
-        dealt = []
+        usuals = []
+        negated = []
         picks = {}
+
+        def turn_x(i, c):
+            b, place = divmod(i, PACK)
+            bank = psum.tile([P, BANK // P, P], F32, name="turn_bank", tag="y")
+            for mb in range(BANK // P):
+                cols = slice(c + mb * P, c + (mb + 1) * P)
+                nc.tensor.matmul(
+                    bank[:, mb], lhsT=usuals[i][:, cols], rhs=identity[:], start=True, stop=False, is_transpose=True
+                )
+                nc.tensor.matmul(
+                    bank[:, mb], lhsT=negated[i][:, cols], rhs=identity[:], start=False, stop=True, is_transpose=True
+                )
+            nc.scalar.activation(
+                x_turned[b][:, c // P : (c + BANK) // P, place * P : (place + 1) * P], bank[:], ACT.Copy, scale=-1.0
+            )
+
+        def quantize_x(b, c):
+            woven = work.tile([P, BANK, PACK], BF16, name="x_woven", align_bytes=64)
+            woven_words = woven[:].rearrange("p m j -> p (m j)").bitcast(F32)
+            for first in range(0, BANK // P, 2):
+                bank = psum.tile([P, 2, 2, P], F32, name="back_bank", tag="y")
+                for mb in range(2):
+                    words = x_turned[b][:, c // P + first + mb, :].bitcast(F32)
+                    for u in range(2):
+                        nc.tensor.transpose(bank[:, mb, u], words[:, u::2], identity[:])
+                nc.scalar.copy(
+                    woven_words[:, first * 2 * P : (first + 2) * 2 * P].rearrange("p (mb m u) -> p mb m u", mb=2, u=2),
+                    bank[:].rearrange("p mb u m -> p mb m u"),
+                )
+            nc.vector.quantize_mx(
+                x_codes[:, b, c : c + BANK].bitcast(FP8X4),
+                x_planes[:, b, c : c + BANK],
+                woven[:].rearrange("p m j -> p (m j)"),
+            )
 
         with tc.tile_pool(name="main_pool", bufs=2) as main_pool:
 
             def load_w1(group, passes=range(K_PASSES)):
                 first, width = sum(W1_GROUPS[:group]), W1_GROUPS[group]
                 if group not in w1_raw:
-                    shape = [P, K_PASSES, PACK, width]
-                    if width == P:
-                        w1_raw[group] = mid(shape, F32, "w1_narrow")
-                    else:
-                        w1_raw[group] = big(shape, F32, "w1_raw_%d" % group)
+                    new_tile = mid if width == P else big
+                    w1_raw[group] = new_tile([P, K_PASSES, PACK, width], F32, "w1_raw_%d" % group)
                 for a in passes:
-                    rows = w1[a * P * PACK : (a + 1) * P * PACK, first : first + width]
+                    rows = w1[a * PASS : (a + 1) * PASS, first : first + width]
                     nc.sync.dma_start(w1_raw[group][:, a], rows.rearrange("(p j) c -> p j c", j=PACK))
 
             def quantize_w1(group):
                 first, width = sum(W1_GROUPS[:group]), W1_GROUPS[group]
                 woven = main_pool.tile([P, K_PASSES, width, PACK], BF16, name="w1_woven", align_bytes=64)
                 for a in range(K_PASSES):
-                    weave(woven[:, a], w1_raw[group][:, a])
+                    nc.scalar.copy(
+                        woven[:, a].rearrange("p (c e) j -> p c j e", e=PACK),
+                        w1_raw[group][:, a].rearrange("p j (c e) -> p c j e", e=PACK),
+                    )
                     codes = keep.tile([P, width], U32, name="w1_codes_%d_%d" % (group, a), align_bytes=64)
                     plane = keep.tile([P, width], U8, name="w1_plane_%d_%d" % (group, a), align_bytes=64)
                     nc.vector.quantize_mx(codes[:].bitcast(FP8X4), plane[:], woven[:, a].rearrange("p c j -> p (c j)"))
@@ -113,9 +154,10 @@ def tile_list_eel_passage_ledger_kernel(
                         w1_planes[(first + c) // P, a] = plane[:, c : c + P]
 
             def put(i, first, count):
-                h = work.tile([P, count], F32, name="h", bufs=3)
-                for c in range(first, first + count, BANK):
-                    n = min(count, BANK)
+                h = main_pool.tile([P, count], F32, name="h", bufs=3)
+                n = min(count, BANK)
+                parts = [h[:, c : c + n] for c in range(0, count, n)]
+                for part, c in zip(parts, range(first, first + count, n)):
                     half, start = divmod(c, BANK)
                     f = psum.tile([P, n], F32, name="f")
                     for a in range(K_PASSES):
@@ -128,8 +170,7 @@ def tile_list_eel_passage_ledger_kernel(
                             start=(a == 0),
                             stop=(a == K_PASSES - 1),
                         )
-                    nc.scalar.activation(h[:, c - first : c - first + n], f[:], ACT.Abs)
-                parts = [h[:, c : c + BANK] for c in range(0, count, BANK)] if count > BANK else [h[:]]
+                    nc.scalar.activation(part, f[:], ACT.Abs)
                 for part in parts:
                     nc.scalar.activation(part, part, ACT.Abs_reciprocal_sqrt, bias=1.0)
                 for part in parts:
@@ -143,17 +184,17 @@ def tile_list_eel_passage_ledger_kernel(
             windows = []
             for a in range(K_PASSES):
                 if a == K_PASSES - 1:
-                    load_w1(0, (1, 2))
+                    load_w1(0, range(1, K_PASSES))
                 window = big([P, T], I32, "window")
                 nc.sync.dma_start(window[:], tab_words[a].rearrange("p t i -> p (t i)").bitcast(I32))
                 windows.append(window)
                 if a == 0:
-                    for quad in range(4):
+                    for quad in range(QUADRANTS):
                         nc.sync.dma_start(
                             tab_planes[32 * quad : 32 * quad + 4 * K_PASSES, :].bitcast(I32),
                             tab_scales[:, 4 * quad : 4 * quad + 4, :].bitcast(I32),
                         )
-                    load_w1(0, (0,))
+                    load_w1(0, range(1))
             quantize_w1(0)
             for a in range(K_PASSES):
                 if a == 1:
@@ -167,79 +208,71 @@ def tile_list_eel_passage_ledger_kernel(
             nc.sync.dma_start(idx2[:], offs2)
 
             for i in range(SLICES):
-                b, quad = divmod(i, PACK)
-                if i < 4:
+                if i < OWN_PAGES:
                     page = keep.tile([P, T2], F32, name="page_%d" % i)
-                elif i < 6:
-                    page = mid([P, T2], F32, "page_%d" % i)
                 else:
-                    page = big([P, T2], F32, "page_%d" % i)
+                    page = (mid if i < SLICES - 2 else big)([P, T2], F32, "page_%d" % i)
                 pages.append(page)
-                nc.sync.dma_start(pages[i][:], page0[i * P : (i + 1) * P, :])
+                nc.sync.dma_start(page[:], page0[i * P : (i + 1) * P, :])
                 if i == 0:
                     for c in range(0, S, BANK):
                         nc.sync.dma_start(wgs_sb[:, c : c + BANK], wgs[:, c : c + BANK])
-                for group in LOADS.get(i, ()):
+                groups = [g for g in range(1, len(W1_GROUPS)) if max(g - W1_AHEAD, 0) == i]
+                for group in groups:
                     load_w1(group)
-                usual_sb = main_pool.tile([P, NP], F32, name="usual_sb", bufs=3)
                 if i == 0:
                     nc.sync.dma_start(idx3[:], offs3)
+                usual_sb = work.tile([P, M], F32, name="usual_sb", bufs=HELD_SLICES)
                 nc.sync.dma_start(usual_sb[:], usual[i * P : (i + 1) * P, :])
+                usuals.append(usual_sb)
                 if i == 0:
                     nc.sync.dma_start(idx4[:], offs4)
                 if i == SLICES - 2:
                     nc.sync.dma_start(w4_sb[:].bitcast(I32), w4_words.rearrange("a p c -> p a c").bitcast(I32))
                     nc.vector.memset(w4_planes[:].bitcast(I32), 0)
-                    for q in range(4):
+                    for quad in range(QUADRANTS):
                         nc.sync.dma_start(
-                            w4_planes[32 * q : 32 * q + 4, :, :].bitcast(I32),
-                            w4_scales[:, 4 * q : 4 * q + 4, :].rearrange("a r c -> r a c").bitcast(I32),
+                            w4_planes[32 * quad : 32 * quad + 4, :, :].bitcast(I32),
+                            w4_scales[:, 4 * quad : 4 * quad + 4, :].rearrange("a r c -> r a c").bitcast(I32),
                         )
                     with nc.allow_non_contiguous_dma(reason="one value for each row of a slice"):
                         nc.sync.dma_start(moon_sb[:], moon.rearrange("(i p) -> p i", p=P))
                     nc.scalar.mul(neg_moon[:], moon_sb[:], -1.0)
-                pieces = ((0, 256), (256, 256), (512, 512)) if i == 0 else ((0, S),)
-                for first, count in pieces:
+                for first, count in FIRST_PIECES if i == 0 else ((0, S),):
                     put(i, first, count)
-                for group in QUANTS.get(i, ()):
+                for group in groups:
                     quantize_w1(group)
-                if i == 0:
-                    dealt.append(keep.tile([P, PACK, NP], F32, name="dealt_0"))
-                if i == PACK:
-                    dealt.append(big([P, PACK, NP], F32, "dealt_1"))
-                pieces = ((0, BANK), (BANK, BANK)) if i == SLICES - 1 else ((0, NP),)
-                queue = nc.sync if i == SLICES - 1 else nc.gpsimd
-                for first, count in pieces:
-                    x = work.tile([P, count], F32, name="x")
-                    nc.vector.tensor_tensor(
-                        x[:],
-                        pages[i][:].indirect(entries(idx3, first, count)),
-                        usual_sb[:, first : first + count],
-                        ALU.subtract,
+                neg = work.tile([P, M], F32, name="negated", bufs=HELD_SLICES)
+                for c in range(0, M, BANK):
+                    nc.vector.tensor_scalar(
+                        neg[:, c : c + BANK], page[:].indirect(entries(idx3, c, BANK)), -1.0, 0.0, ALU.mult, ALU.add
                     )
-                    queue.dma_start(dealt[b][32 * quad : 32 * quad + 32, :, first : first + count], x[:])
-                if i < EARLY:
-                    g = keep.tile([P, NP], F32, name="g_%d" % i)
-                    nc.vector.tensor_copy(g[:], pages[i][:].indirect(idx4[:]))
-                    for c in range(0, NP, BANK):
-                        picks[i, c] = g[:, c : c + BANK]
+                negated.append(neg)
+                if i == 0:
+                    first_picks = keep.tile([P, M], F32, name="first_picks")
+                    nc.vector.tensor_copy(first_picks[:], page[:].indirect(idx4[:]))
+                    for c in range(0, M, BANK):
+                        picks[i, c] = first_picks[:, c : c + BANK]
+                if i >= TURN_LAG:
+                    for c in range(0, M, BANK):
+                        turn_x(i - TURN_LAG, c)
+                if i == PACK + TURN_LAG:
+                    for c in range(0, M, BANK):
+                        quantize_x(0, c)
 
         with tc.tile_pool(name="tail_pool", bufs=2) as tail_pool:
-            for c in range(0, NP, BANK):
-                for b in range(R_PASSES):
-                    woven = tail_pool.tile([P, BANK, PACK], BF16, name="x_woven", bufs=4, align_bytes=64)
-                    weave(woven[:], dealt[b][:, :, c : c + BANK])
-                    nc.vector.quantize_mx(
-                        x_codes[:, b, c : c + BANK].bitcast(FP8X4),
-                        x_planes[:, b, c : c + BANK],
-                        woven[:].rearrange("p c j -> p (c j)"),
-                    )
-            for c in range(0, NP, BANK):
+            for i in range(SLICES - TURN_LAG, SLICES - 1):
+                for c in range(0, M, BANK):
+                    turn_x(i, c)
+            for c in range(0, M, BANK):
+                turn_x(SLICES - 1, c)
+                quantize_x(R_PASSES - 1, c)
+            for c in range(0, M, BANK):
                 for i in range(SLICES):
                     if (i, c) not in picks:
-                        g = tail_pool.tile([P, BANK], F32, name="g", bufs=TAIL_PICKS)
-                        nc.vector.tensor_copy(g[:], pages[i][:].indirect(entries(idx4, c, BANK)))
-                        picks[i, c] = g[:]
+                        pick = tail_pool.tile([P, BANK], F32, name="pick", bufs=PICK_BUFS)
+                        nc.vector.tensor_copy(pick[:], pages[i][:].indirect(entries(idx4, c, BANK)))
+                        picks[i, c] = pick[:]
                     y = psum.tile([P, BANK], F32, name="y")
                     for b in range(R_PASSES):
                         nc.tensor.matmul_mx(
@@ -251,16 +284,15 @@ def tile_list_eel_passage_ledger_kernel(
                             start=(b == 0),
                             stop=(b == R_PASSES - 1),
                         )
-                    diff = work.tile([P, BANK], F32, name="diff", tag="h", bufs=3)
+                    moon_i = moon_sb[:, i : i + 1]
+                    diff = work.tile([P, BANK], F32, name="diff", tag="negated", bufs=HELD_SLICES)
                     nc.vector.scalar_tensor_tensor(
                         diff[:], picks[i, c], neg_moon[:, i : i + 1], y[:], ALU.mult, ALU.add
                     )
                     res = tail_pool.tile([P, BANK], F32, name="res", bufs=4)
-                    if c * SLICES // BANK + i >= 2 * SLICES - LAST_ON_VECTOR:
-                        nc.vector.scalar_tensor_tensor(
-                            res[:], picks[i, c], moon_sb[:, i : i + 1], diff[:], ALU.mult, ALU.mult
-                        )
+                    if c == M - BANK and i >= SLICES - LAST_ON_VECTOR:
+                        nc.vector.scalar_tensor_tensor(res[:], picks[i, c], moon_i, diff[:], ALU.mult, ALU.mult)
                     else:
                         nc.gpsimd.tensor_tensor(res[:], diff[:], picks[i, c], ALU.mult)
-                        nc.scalar.activation(res[:], res[:], ACT.Copy, scale=moon_sb[:, i : i + 1])
+                        nc.scalar.activation(res[:], res[:], ACT.Copy, scale=moon_i)
                     nc.sync.dma_start(out[i * P : (i + 1) * P, c : c + BANK], res[:])

from contextlib import ExitStack

import concourse.mybir as mybir
from concourse.masks import make_identity

K, H, T, S, T2, M = 1536, 1024, 4096, 1024, 2048, 1024
FLOPS = 2 * K * H * S + 2 * H * H * M

F32 = mybir.dt.float32
BF16 = mybir.dt.bfloat16
I32 = mybir.dt.int32
U32 = mybir.dt.uint32
U16 = mybir.dt.uint16
U8 = mybir.dt.uint8
FP8X4 = mybir.dt.float8_e4m3fn_x4
FP4X4 = mybir.dt.float4_e2m1fn_x4
ALU = mybir.AluOpType
ACT = mybir.ActivationFunctionType

P = 128
PACK = 4
PASS = P * PACK
BANK = 512
QUADRANTS = 4
LIST_ROWS = 16
K_PASSES = K // PASS
R_PASSES = H // PASS
SLICES = H // P

W1_GROUPS = (P, P, P, P, 2 * P, 2 * P)
W1_AHEAD = 2
FIRST_PIECES = ((0, BANK // 2), (BANK // 2, BANK // 2), (BANK, BANK))
TURN_LAG = 2
PICK_BUFS = 6
LAST_ON_VECTOR = 2
OWN_PAGES = 4
MID_BUFS = 4
HELD_SLICES = TURN_LAG + 1


def tile_list_eel_passage_ledger_kernel(
    tc, tab_words, tab_scales, offs, offs2, offs3, offs4, w1, gain, wgs, page0, usual, w4_words, w4_scales, moon, out
):
    nc = tc.nc
    with ExitStack() as ctx:
        keep = ctx.enter_context(tc.tile_pool(name="keep", bufs=1))
        work = ctx.enter_context(tc.tile_pool(name="work", bufs=2))
        psum = ctx.enter_context(tc.psum_pool(name="psum", bufs=4))

        def entries(lst, first, count):
            return lst[:, first // LIST_ROWS : (first + count) // LIST_ROWS]

        def big(shape, dtype, name):
            return work.tile(shape, dtype, name=name, tag="big", bufs=K_PASSES)

        def mid(shape, dtype, name):
            return work.tile(shape, dtype, name=name, tag="mid", bufs=MID_BUFS)

        idx1 = keep.tile([P, S // LIST_ROWS], U16, name="idx1")
        idx2 = keep.tile([P, S // LIST_ROWS], U16, name="idx2")
        idx3 = keep.tile([P, M // LIST_ROWS], U16, name="idx3")
        idx4 = keep.tile([P, M // LIST_ROWS], U16, name="idx4")
        nc.sync.dma_start(idx1[:], offs)

        ones = keep.tile([P, 8], F32, name="ones")
        warmed = keep.tile([P, 8], F32, name="warmed")
        nc.vector.memset(ones[:], 1.0)
        nc.scalar.activation(warmed[:], ones[:], ACT.Abs_reciprocal_sqrt)

        tab_planes = work.tile([P, T], U8, name="tab_planes", tag="negated", bufs=HELD_SLICES)
        nc.vector.memset(tab_planes[:].bitcast(I32), 0)
        identity = keep.tile([P, P], F32, name="identity")
        make_identity(nc, identity[:])

        gain_sb = keep.tile([P, SLICES], F32, name="gain_sb")
        moon_sb = keep.tile([P, SLICES], F32, name="moon_sb")
        neg_moon = keep.tile([P, SLICES], F32, name="neg_moon")
        with nc.allow_non_contiguous_dma(reason="one value for each row of a slice"):
            nc.scalar.dma_start(gain_sb[:], gain.rearrange("(i p) -> p i", p=P))
        wgs_sb = keep.tile([P, S], F32, name="wgs_sb")
        v_planes = keep.tile([P, S], U8, name="v_planes", align_bytes=64)
        x_turned = [keep.tile([P, M // P, PASS], BF16, name="x_turned_%d" % b) for b in range(R_PASSES)]
        x_codes = keep.tile([P, R_PASSES, M], U32, name="x_codes", align_bytes=64)
        x_planes = keep.tile([P, R_PASSES, M], U8, name="x_planes", align_bytes=64)
        w4_sb = keep.tile([P, R_PASSES, 2 * H], U8, name="w4_sb", align_bytes=64)
        w4_planes = keep.tile([P, R_PASSES, H], U8, name="w4_planes", align_bytes=64)
        w1_raw = {}
        w1_codes = {}
        w1_planes = {}
        v_codes = {}
        pages = []
        usuals = []
        negated = []
        picks = {}

        def turn_x(i, c):
            b, place = divmod(i, PACK)
            bank = psum.tile([P, BANK // P, P], F32, name="turn_bank", tag="y")
            for mb in range(BANK // P):
                cols = slice(c + mb * P, c + (mb + 1) * P)
                nc.tensor.matmul(
                    bank[:, mb], lhsT=usuals[i][:, cols], rhs=identity[:], start=True, stop=False, is_transpose=True
                )
                nc.tensor.matmul(
                    bank[:, mb], lhsT=negated[i][:, cols], rhs=identity[:], start=False, stop=True, is_transpose=True
                )
            nc.scalar.activation(
                x_turned[b][:, c // P : (c + BANK) // P, place * P : (place + 1) * P], bank[:], ACT.Copy, scale=-1.0
            )

        def quantize_x(b, c):
            woven = work.tile([P, BANK, PACK], BF16, name="x_woven", align_bytes=64)
            woven_words = woven[:].rearrange("p m j -> p (m j)").bitcast(F32)
            for first in range(0, BANK // P, 2):
                bank = psum.tile([P, 2, 2, P], F32, name="back_bank", tag="y")
                for mb in range(2):
                    words = x_turned[b][:, c // P + first + mb, :].bitcast(F32)
                    for u in range(2):
                        nc.tensor.transpose(bank[:, mb, u], words[:, u::2], identity[:])
                nc.scalar.copy(
                    woven_words[:, first * 2 * P : (first + 2) * 2 * P].rearrange("p (mb m u) -> p mb m u", mb=2, u=2),
                    bank[:].rearrange("p mb u m -> p mb m u"),
                )
            nc.vector.quantize_mx(
                x_codes[:, b, c : c + BANK].bitcast(FP8X4),
                x_planes[:, b, c : c + BANK],
                woven[:].rearrange("p m j -> p (m j)"),
            )

        with tc.tile_pool(name="main_pool", bufs=2) as main_pool:

            def load_w1(group, passes=range(K_PASSES)):
                first, width = sum(W1_GROUPS[:group]), W1_GROUPS[group]
                if group not in w1_raw:
                    new_tile = mid if width == P else big
                    w1_raw[group] = new_tile([P, K_PASSES, PACK, width], F32, "w1_raw_%d" % group)
                for a in passes:
                    rows = w1[a * PASS : (a + 1) * PASS, first : first + width]
                    nc.sync.dma_start(w1_raw[group][:, a], rows.rearrange("(p j) c -> p j c", j=PACK))

            def quantize_w1(group):
                first, width = sum(W1_GROUPS[:group]), W1_GROUPS[group]
                woven = main_pool.tile([P, K_PASSES, width, PACK], BF16, name="w1_woven", align_bytes=64)
                for a in range(K_PASSES):
                    nc.scalar.copy(
                        woven[:, a].rearrange("p (c e) j -> p c j e", e=PACK),
                        w1_raw[group][:, a].rearrange("p j (c e) -> p c j e", e=PACK),
                    )
                    codes = keep.tile([P, width], U32, name="w1_codes_%d_%d" % (group, a), align_bytes=64)
                    plane = keep.tile([P, width], U8, name="w1_plane_%d_%d" % (group, a), align_bytes=64)
                    nc.vector.quantize_mx(codes[:].bitcast(FP8X4), plane[:], woven[:, a].rearrange("p c j -> p (c j)"))
                    for c in range(0, width, P):
                        w1_codes[(first + c) // P, a] = codes[:, c : c + P]
                        w1_planes[(first + c) // P, a] = plane[:, c : c + P]

            def put(i, first, count):
                h = main_pool.tile([P, count], F32, name="h", bufs=3)
                n = min(count, BANK)
                parts = [h[:, c : c + n] for c in range(0, count, n)]
                for part, c in zip(parts, range(first, first + count, n)):
                    half, start = divmod(c, BANK)
                    f = psum.tile([P, n], F32, name="f")
                    for a in range(K_PASSES):
                        nc.tensor.matmul_mx(
                            out=f[:],
                            lhsT=w1_codes[i, a].bitcast(FP8X4),
                            lhsT_scale=w1_planes[i, a],
                            rhs=v_codes[a, half][:, start : start + n].bitcast(FP8X4),
                            rhs_scale=v_planes[4 * a :, c : c + n],
                            start=(a == 0),
                            stop=(a == K_PASSES - 1),
                        )
                    nc.scalar.activation(part, f[:], ACT.Abs)
                for part in parts:
                    nc.scalar.activation(part, part, ACT.Abs_reciprocal_sqrt, bias=1.0)
                for part in parts:
                    nc.scalar.activation(part, part, ACT.Square)
                for part in parts:
                    nc.scalar.activation(part, part, ACT.Copy, scale=gain_sb[:, i : i + 1])
                nc.vector.tensor_tensor(
                    pages[i][:].indirect(entries(idx2, first, count)), h[:], wgs_sb[:, first : first + count], ALU.mult
                )

            windows = []
            for a in range(K_PASSES):
                if a == K_PASSES - 1:
                    load_w1(0, range(1, K_PASSES))
                window = big([P, T], I32, "window")
                nc.sync.dma_start(window[:], tab_words[a].rearrange("p t i -> p (t i)").bitcast(I32))
                windows.append(window)
                if a == 0:
                    for quad in range(QUADRANTS):
                        nc.sync.dma_start(
                            tab_planes[32 * quad : 32 * quad + 4 * K_PASSES, :].bitcast(I32),
                            tab_scales[:, 4 * quad : 4 * quad + 4, :].bitcast(I32),
                        )
                    load_w1(0, range(1))
            quantize_w1(0)
            for a in range(K_PASSES):
                if a == 1:
                    nc.vector.tensor_copy(v_planes[:], tab_planes[:].indirect(idx1[:]))
                for half in range(S // BANK):
                    picked = keep.tile([P, BANK], U32, name="v_codes_%d_%d" % (a, half), align_bytes=64)
                    nc.vector.tensor_copy(
                        picked[:], windows[a][:].bitcast(U32).indirect(entries(idx1, half * BANK, BANK))
                    )
                    v_codes[a, half] = picked
            nc.sync.dma_start(idx2[:], offs2)

            for i in range(SLICES):
                if i < OWN_PAGES:
                    page = keep.tile([P, T2], F32, name="page_%d" % i)
                else:
                    page = (mid if i < SLICES - 2 else big)([P, T2], F32, "page_%d" % i)
                pages.append(page)
                nc.sync.dma_start(page[:], page0[i * P : (i + 1) * P, :])
                if i == 0:
                    for c in range(0, S, BANK):
                        nc.sync.dma_start(wgs_sb[:, c : c + BANK], wgs[:, c : c + BANK])
                groups = [g for g in range(1, len(W1_GROUPS)) if max(g - W1_AHEAD, 0) == i]
                for group in groups:
                    load_w1(group)
                if i == 0:
                    nc.sync.dma_start(idx3[:], offs3)
                usual_sb = work.tile([P, M], F32, name="usual_sb", bufs=HELD_SLICES)
                nc.sync.dma_start(usual_sb[:], usual[i * P : (i + 1) * P, :])
                usuals.append(usual_sb)
                if i == 0:
                    nc.sync.dma_start(idx4[:], offs4)
                if i == SLICES - 2:
                    nc.sync.dma_start(w4_sb[:].bitcast(I32), w4_words.rearrange("a p c -> p a c").bitcast(I32))
                    nc.vector.memset(w4_planes[:].bitcast(I32), 0)
                    for quad in range(QUADRANTS):
                        nc.sync.dma_start(
                            w4_planes[32 * quad : 32 * quad + 4, :, :].bitcast(I32),
                            w4_scales[:, 4 * quad : 4 * quad + 4, :].rearrange("a r c -> r a c").bitcast(I32),
                        )
                    with nc.allow_non_contiguous_dma(reason="one value for each row of a slice"):
                        nc.sync.dma_start(moon_sb[:], moon.rearrange("(i p) -> p i", p=P))
                    nc.scalar.mul(neg_moon[:], moon_sb[:], -1.0)
                for first, count in FIRST_PIECES if i == 0 else ((0, S),):
                    put(i, first, count)
                for group in groups:
                    quantize_w1(group)
                neg = work.tile([P, M], F32, name="negated", bufs=HELD_SLICES)
                for c in range(0, M, BANK):
                    nc.vector.tensor_scalar(
                        neg[:, c : c + BANK], page[:].indirect(entries(idx3, c, BANK)), -1.0, 0.0, ALU.mult, ALU.add
                    )
                negated.append(neg)
                if i == 0:
                    first_picks = keep.tile([P, M], F32, name="first_picks")
                    nc.vector.tensor_copy(first_picks[:], page[:].indirect(idx4[:]))
                    for c in range(0, M, BANK):
                        picks[i, c] = first_picks[:, c : c + BANK]
                if i >= TURN_LAG:
                    for c in range(0, M, BANK):
                        turn_x(i - TURN_LAG, c)
                if i == PACK + TURN_LAG:
                    for c in range(0, M, BANK):
                        quantize_x(0, c)

        with tc.tile_pool(name="tail_pool", bufs=2) as tail_pool:
            for i in range(SLICES - TURN_LAG, SLICES - 1):
                for c in range(0, M, BANK):
                    turn_x(i, c)
            for c in range(0, M, BANK):
                turn_x(SLICES - 1, c)
                quantize_x(R_PASSES - 1, c)
            for c in range(0, M, BANK):
                for i in range(SLICES):
                    if (i, c) not in picks:
                        pick = tail_pool.tile([P, BANK], F32, name="pick", bufs=PICK_BUFS)
                        nc.vector.tensor_copy(pick[:], pages[i][:].indirect(entries(idx4, c, BANK)))
                        picks[i, c] = pick[:]
                    y = psum.tile([P, BANK], F32, name="y")
                    for b in range(R_PASSES):
                        nc.tensor.matmul_mx(
                            out=y[:],
                            lhsT=w4_sb[:, b, 2 * i * P : 2 * (i + 1) * P].bitcast(FP4X4),
                            lhsT_scale=w4_planes[:, b, i * P : (i + 1) * P],
                            rhs=x_codes[:, b, c : c + BANK].bitcast(FP8X4),
                            rhs_scale=x_planes[:, b, c : c + BANK],
                            start=(b == 0),
                            stop=(b == R_PASSES - 1),
                        )
                    moon_i = moon_sb[:, i : i + 1]
                    diff = work.tile([P, BANK], F32, name="diff", tag="negated", bufs=HELD_SLICES)
                    nc.vector.scalar_tensor_tensor(
                        diff[:], picks[i, c], neg_moon[:, i : i + 1], y[:], ALU.mult, ALU.add
                    )
                    res = tail_pool.tile([P, BANK], F32, name="res", bufs=4)
                    if c == M - BANK and i >= SLICES - LAST_ON_VECTOR:
                        nc.vector.scalar_tensor_tensor(res[:], picks[i, c], moon_i, diff[:], ALU.mult, ALU.mult)
                    else:
                        nc.gpsimd.tensor_tensor(res[:], diff[:], picks[i, c], ALU.mult)
                        nc.scalar.activation(res[:], res[:], ACT.Copy, scale=moon_i)
                    nc.sync.dma_start(out[i * P : (i + 1) * P, c : c + BANK], res[:])
